import numpy as np
import ml_dtypes


def mxq(x, axis, fmt="e4m3"):
    dtype, down = {"e4m3": (ml_dtypes.float8_e4m3fn, 7), "e5m2": (ml_dtypes.float8_e5m2, 14)}[fmt]
    v = np.moveaxis(np.asarray(x, np.float32).astype(ml_dtypes.bfloat16).astype(np.float64), axis, -1)
    blocks = v.reshape(v.shape[:-1] + (-1, 32))
    amax = np.abs(blocks).max(-1, keepdims=True)
    byte = np.maximum(np.where(amax > 0, np.frexp(amax)[1] - 1 + 127, 0) - down, 1)
    scale = np.exp2(byte - 127.0)
    codes = (blocks / scale).astype(np.float32).astype(dtype).astype(np.float64)
    return np.moveaxis((codes * scale).reshape(v.shape), -1, axis)


WIDE = False


def mx_kscale(k):
    if not WIDE:
        return np.ones(k)
    levels = np.array([30, -30])
    if k % 512:
        return np.exp2(np.random.permutation(np.resize(levels, k // 32))).repeat(32)
    a = np.empty((k // 512, 16))
    for p in range(k // 512):
        a[p, :8] = np.random.permutation(np.resize(levels, 8))
        for g in range(8):
            far = levels[np.abs(levels - a[p, g]) >= 10]
            a[p, g + 8] = far[np.random.randint(len(far))]
    return np.exp2(a.ravel()).repeat(32)


def f64(x):
    return np.asarray(x).astype(np.float64)


E2M1 = np.array([0.0, 0.5, 1.0, 1.5, 2.0, 3.0, 4.0, 6.0, -0.0, -0.5, -1.0, -1.5, -2.0, -3.0, -4.0, -6.0])


def pack_weight(w, fmt):
    k, n = w.shape
    w = f64(np.asarray(w, np.float32).astype(ml_dtypes.bfloat16)).reshape(k // 32, 32, n)
    amax = np.abs(w).max(1)
    if fmt == "e4m3":
        byte = np.frexp(amax)[1] - 1 + 127 - 7
    else:
        mant, ex = np.frexp(amax / 6.0)
        byte = np.where(mant > 0.5, ex, ex - 1) + 127
    byte = np.clip(np.where(amax > 0, byte, 1), 1, 254)
    scaled = (w * np.exp2(127.0 - byte)[:, None, :]).reshape(k, n).astype(np.float32)
    by_word = np.ascontiguousarray(scaled.reshape(k // 512, 128, 4, n).transpose(0, 1, 3, 2))
    if fmt == "e4m3":
        words = by_word.astype(ml_dtypes.float8_e4m3fn).view(np.uint8)
    else:
        c = by_word.astype(ml_dtypes.float4_e2m1fn).view(np.uint8) & 0xF
        words = (c[..., 0::2] | (c[..., 1::2] << 4)).reshape(k // 512, 128, 2 * n)
    return np.ascontiguousarray(words), np.ascontiguousarray(byte.astype(np.uint8).reshape(k // 512, 16, n))


def unpack_weight(words, scales, fmt):
    g, _, n = scales.shape
    words = np.ascontiguousarray(words).reshape(g, 128, n, -1)
    if fmt == "e4m3":
        vals = words.view(ml_dtypes.float8_e4m3fn).astype(np.float64)
    else:
        nib = np.empty((g, 128, n, 4), np.uint8)
        nib[..., 0::2] = words & 0xF
        nib[..., 1::2] = words >> 4
        vals = E2M1[nib]
    vals = vals * np.repeat(np.exp2(scales.astype(np.float64) - 127.0), 8, axis=1)[..., None]
    return vals.transpose(0, 1, 3, 2).reshape(g * 512, n)


N, R, K, T = 1024, 512, 512, 512


def setup_inputs():
    n = np.random.standard_normal
    fn = mx_kscale(N)
    fr = mx_kscale(R)
    wdp = pack_weight(n((N, R)) * 1 / np.sqrt(N) * fn[:, None], "e2m1")
    wap = pack_weight(n((R, K)) * 1 / np.sqrt(R) / fr[:, None], "e4m3")
    wbp = pack_weight(n((R, K)) * 1 / np.sqrt(R) / fr[:, None], "e2m1")
    return {
        "g": (n((N, T)) * np.exp(0.5 * n((1, T))) / fn[:, None]).astype(np.float32),
        "wd_words": wdp[0],
        "wd_scales": wdp[1],
        "gs": (np.random.uniform(0.05, 0.95, (R, T)) * fr[:, None]).astype(np.float32),
        "zs": (n((R, T)) * fr[:, None]).astype(np.float32),
        "wa_words": wap[0],
        "wa_scales": wap[1],
        "wb_words": wbp[0],
        "wb_scales": wbp[1],
    }


def reference(g, wd_words, wd_scales, gs, zs, wa_words, wa_scales, wb_words, wb_scales):
    wdu = unpack_weight(wd_words, wd_scales, "e2m1")
    wau = unpack_weight(wa_words, wa_scales, "e4m3")
    wbu = unpack_weight(wb_words, wb_scales, "e2m1")
    gq = mxq(f64(g), 0, "e5m2")
    d = wdu.T @ gq
    da = d * f64(gs)
    db = d * f64(zs)
    daq = mxq(da, 0, "e5m2")
    dbq = mxq(db, 0, "e4m3")
    y = wau.T @ daq + wbu.T @ dbq
    return y

@@ -1,0 +1,291 @@
+from contextlib import ExitStack
+
+import concourse.mybir as mybir
+from concourse.masks import make_identity
+
+N, R, K, T = 1024, 512, 512, 512
+FLOPS = 2 * N * R * T + 2 * 2 * R * K * T
+
+F32 = mybir.dt.float32
+BF16 = mybir.dt.bfloat16
+I32 = mybir.dt.int32
+U32 = mybir.dt.uint32
+U8 = mybir.dt.uint8
+E4M3 = mybir.dt.float8_e4m3fn_x4
+E5M2 = mybir.dt.float8_e5m2_x4
+E2M1 = mybir.dt.float4_e2m1fn_x4
+MULT = mybir.AluOpType.mult
+
+P = 128
+PACK = 4
+TT = 128
+RUN = 4
+HALF = 256
+
+
+def tile_mix_gradient_of_gated_sum_kernel(tc, g, wd_words, wd_scales, gs, zs, wa_words, wa_scales, wb_words, wb_scales, out):
+    nc = tc.nc
+    with ExitStack() as ctx:
+        sb = ctx.enter_context(tc.tile_pool(name="sb", bufs=1))
+        ps = ctx.enter_context(tc.psum_pool(name="ps", bufs=1))
+        ctx.enter_context(tc.manual_schedule())
+
+        wd = sb.tile([P, 2 * 2 * R], U8, name="wd", align_bytes=64)
+        wa = sb.tile([P, K], U32, name="wa", align_bytes=64)
+        wb = sb.tile([P, 2 * K], U8, name="wb", align_bytes=64)
+        wd_s = sb.tile([P, 2 * R], U8, name="wd_s", align_bytes=64)
+        wa_s = sb.tile([P, K], U8, name="wa_s", align_bytes=64)
+        wb_s = sb.tile([P, K], U8, name="wb_s", align_bytes=64)
+        da_q = sb.tile([P, 5 * HALF], U32, name="da_q", align_bytes=64)
+        da_s = sb.tile([P, 5 * HALF], U8, name="da_s", align_bytes=64)
+        db_q = sb.tile([P, T], U32, name="db_q", align_bytes=64)
+        db_s = sb.tile([P, T], U8, name="db_s", align_bytes=64)
+        ident = sb.tile([P, P], F32, name="ident", align_bytes=64)
+
+        nc.vector.memset(wd_s[:].bitcast(I32), 0)
+        nc.vector.memset(wa_s[:].bitcast(I32), 0)
+        nc.vector.memset(wb_s[:].bitcast(I32), 0)
+        make_identity(nc, ident[:])
+        for pad in range(3):
+            nc.vector.memset(da_q[:, 2 * pad * HALF : (2 * pad + 1) * HALF], 0)
+        nc.vector.memset(da_s[:].bitcast(I32), 0)
+
+        g_raw = {}
+        fac = {}
+
+        def load_g(c, z):
+            t = sb.tile([P, PACK, TT], F32, name=f"g_raw{c}{z}", align_bytes=64)
+            src = g[z * 512 : (z + 1) * 512, c * TT : (c + 1) * TT]
+            nc.sync.dma_start(out=t[:], in_=src.rearrange("(p j) t -> p j t", j=PACK))
+            g_raw[c, z] = t
+
+        def load_fac(key, c0, n):
+            src = {"a": gs, "b": zs}[key]
+            t = sb.tile([P, PACK, n * TT], F32, name=f"fac{key}{c0}", align_bytes=64)
+            nc.sync.dma_start(out=t[:], in_=src[:, c0 * TT : (c0 + n) * TT].rearrange("(p j) t -> p j t", j=PACK))
+            for i in range(n):
+                fac[key, c0 + i] = t[:, :, i * TT : (i + 1) * TT]
+
+        def load_scale(key, r, eng):
+            plane, src = {"d": (wd_s, wd_scales), "a": (wa_s, wa_scales), "b": (wb_s, wb_scales)}[key]
+            z = src.shape[0]
+            dst = plane[:].bitcast(I32)[r:P:32, :].rearrange("q (z n) -> q z n", z=z)
+            eng.dma_start(out=dst, in_=src.bitcast(I32).rearrange("z (q r) n -> r q z n", r=4)[r])
+
+        def load_w(key):
+            if key == "d":
+                nc.sync.dma_start(out=wd[:].bitcast(I32).rearrange("p (z n) -> p z n", z=2), in_=wd_words.bitcast(I32).rearrange("z p n -> p z n"))
+            elif key == "a":
+                nc.sync.dma_start(out=wa[:].bitcast(I32), in_=wa_words[0].rearrange("p n j -> p (n j)").bitcast(I32))
+            else:
+                nc.sync.dma_start(out=wb[:].bitcast(I32), in_=wb_words[0].bitcast(I32))
+
+        load_g(0,0)
+        load_g(0,1)
+        load_w("d")
+        load_scale("d",0,nc.sync)
+        load_scale("d",1,nc.sync)
+        load_scale("d",2,nc.sync)
+        load_scale("d",3,nc.sync)
+        load_g(1,0)
+        load_g(1,1)
+        load_g(2,0)
+        load_g(2,1)
+        load_fac("a",0,1)
+        load_g(3,0)
+        load_g(3,1)
+        load_fac("b",0,1)
+        load_scale("a",0,nc.sync)
+        load_fac("a",1,1)
+        load_scale("a",1,nc.sync)
+        load_fac("b",1,1)
+        load_scale("a",2,nc.sync)
+        load_w("a")
+        load_scale("a",3,nc.sync)
+        load_fac("a",2,1)
+        load_scale("b",0,nc.sync)
+        load_fac("a",3,1)
+        load_scale("b",1,nc.sync)
+        load_w("b")
+        load_scale("b",2,nc.sync)
+        load_fac("b",2,1)
+        load_scale("b",3,nc.sync)
+        load_fac("b",3,1)
+
+        g_bf = [sb.tile([P, 2 * TT * PACK], BF16, name=f"g_bf{c}", align_bytes=64) for c in range(4)]
+        g_q = [sb.tile([P, 2 * TT], U32, name=f"g_q{c}", align_bytes=64) for c in range(4)]
+        g_s = [sb.tile([P, 2 * TT], U8, name=f"g_s{c}", align_bytes=64) for c in range(4)]
+        dT_ps = {}
+        dT_sb = {}
+        d_ps = {}
+        prod = {}
+        o_ps = {}
+
+        def cast(c, z, eng):
+            dst = g_bf[c][:, z * 512 : (z + 1) * 512].rearrange("p (c i j) -> p c j i", i=RUN, j=PACK)
+            src = g_raw[c, z][:].rearrange("p j (c i) -> p c j i", i=RUN)
+            if eng == "v":
+                nc.vector.tensor_copy(out=dst, in_=src)
+            else:
+                nc.scalar.copy(out=dst, in_=src)
+
+        def qg(c):
+            nc.vector.quantize_mx(out=g_q[c][:].bitcast(E5M2), scales=g_s[c][:], in_=g_bf[c][:])
+
+        def qz(c, z):
+            nc.vector.quantize_mx(out=g_q[c][:, z * TT : (z + 1) * TT].bitcast(E5M2), scales=g_s[c][:, z * TT : (z + 1) * TT], in_=g_bf[c][:, z * 512 : (z + 1) * 512])
+
+        def mz(c, z):
+            if z == 0:
+                dT_ps[c] = ps.tile([P, R], F32, name=f"dT{c}", tag=f"bank{c}")
+            nc.tensor.matmul_mx(
+                out=dT_ps[c][:],
+                lhsT=g_q[c][:, z * TT : (z + 1) * TT].bitcast(E5M2),
+                lhsT_scale=g_s[c][:, z * TT : (z + 1) * TT],
+                rhs=wd[:, z * 2 * R : (z + 1) * 2 * R].bitcast(E2M1),
+                rhs_scale=wd_s[:, z * R : (z + 1) * R],
+                start=(z == 0),
+                stop=(z == 1),
+            )
+
+        def m1(c):
+            acc = ps.tile([P, R], F32, name=f"dT{c}", tag=f"bank{c}")
+            for z in range(2):
+                nc.tensor.matmul_mx(
+                    out=acc[:],
+                    lhsT=g_q[c][:, z * TT : (z + 1) * TT].bitcast(E5M2),
+                    lhsT_scale=g_s[c][:, z * TT : (z + 1) * TT],
+                    rhs=wd[:, z * 2 * R : (z + 1) * 2 * R].bitcast(E2M1),
+                    rhs_scale=wd_s[:, z * R : (z + 1) * R],
+                    start=(z == 0),
+                    stop=(z == 1),
+                )
+            dT_ps[c] = acc
+
+        def ev(c):
+            t = sb.tile([P, PACK, P], F32, name=f"dT_sb{c}", align_bytes=64)
+            nc.scalar.copy(out=t[:], in_=dT_ps[c][:].rearrange("t (m j) -> t j m", j=PACK))
+            dT_sb[c] = t
+
+        def tr(c):
+            acc = ps.tile([P, PACK, TT], F32, name=f"d{c}", tag=f"d{c}")
+            for j in range(PACK):
+                nc.tensor.transpose(acc[:, j, :], dT_sb[c][:, j, :], ident[:])
+            d_ps[c] = acc
+
+        def mul(key, c):
+            t = sb.tile([P, TT * PACK], BF16, name=f"prod{key}{c}", align_bytes=64)
+            nc.vector.tensor_tensor(
+                out=t[:].rearrange("p (c i j) -> p c j i", i=RUN, j=PACK),
+                in0=d_ps[c][:].rearrange("p j (c i) -> p c j i", i=RUN),
+                in1=fac[key, c].rearrange("p j (c i) -> p c j i", i=RUN),
+                op=MULT,
+            )
+            prod[key, c] = t
+
+        def q(key, c):
+            if key == "a":
+                c0 = (2 * (c // 2) + 1) * HALF + (c % 2) * TT
+                nc.vector.quantize_mx(out=da_q[:, c0 : c0 + TT].bitcast(E5M2), scales=da_s[:, c0 : c0 + TT], in_=prod[key, c][:])
+            else:
+                c0 = c * TT
+                nc.vector.quantize_mx(out=db_q[:, c0 : c0 + TT].bitcast(E4M3), scales=db_s[:, c0 : c0 + TT], in_=prod[key, c][:])
+
+        def mA(h, b):
+            acc = ps.tile([P, 2 * HALF], F32, name=f"o{h}{b}", tag=f"bank{2 * h + b}")
+            o_ps[h, b] = acc
+            for a in range(2):
+                kt = 2 * b + a
+                w0 = (2 * h + 1 - a) * HALF
+                nc.tensor.matmul_mx(
+                    out=acc[:],
+                    lhsT=wa[:, kt * P : (kt + 1) * P].bitcast(E4M3),
+                    lhsT_scale=wa_s[:, kt * P : (kt + 1) * P],
+                    rhs=da_q[:, w0 : w0 + 2 * HALF].bitcast(E5M2),
+                    rhs_scale=da_s[:, w0 : w0 + 2 * HALF],
+                    start=(a == 0),
+                    stop=False,
+                )
+
+        def mB(c, b):
+            h = c // 2
+            for a in range(2):
+                kt = 2 * b + a
+                c0 = a * HALF + (c % 2) * TT
+                nc.tensor.matmul_mx(
+                    out=o_ps[h, b][:, c0 : c0 + TT],
+                    lhsT=wb[:, kt * 2 * P : (kt + 1) * 2 * P].bitcast(E2M1),
+                    lhsT_scale=wb_s[:, kt * P : (kt + 1) * P],
+                    rhs=db_q[:, c * TT : (c + 1) * TT].bitcast(E4M3),
+                    rhs_scale=db_s[:, c * TT : (c + 1) * TT],
+                    start=False,
+                    stop=(c % 2 == 1 and a == 1),
+                )
+
+        def fin(h, b, eng, queue):
+            res = sb.tile([P, 2 * HALF], F32, name=f"res{h}{b}", align_bytes=64)
+            if eng == "v":
+                nc.vector.tensor_copy(out=res[:], in_=o_ps[h, b][:])
+            else:
+                nc.scalar.copy(out=res[:], in_=o_ps[h, b][:])
+            dst = out.rearrange("(a p) t -> p a t", p=P)[:, 2 * b : 2 * b + 2, h * HALF : (h + 1) * HALF]
+            queue.dma_start(out=dst, in_=res[:].rearrange("p (a t) -> p a t", a=2))
+
+        cast(0,0,"v")
+        qz(0,0)
+        cast(0,1,"v")
+        mz(0,0)
+        qz(0,1)
+        mz(0,1)
+        cast(1,0,"s")
+        cast(1,1,"v")
+        ev(0)
+        qg(1)
+        cast(2,0,"v")
+        tr(0)
+        m1(1)
+        cast(2,1,"v")
+        qg(2)
+        ev(1)
+        m1(2)
+        mul("a",0)
+        cast(3,0,"s")
+        cast(3,1,"v")
+        tr(1)
+        q("a",0)
+        qg(3)
+        ev(2)
+        m1(3)
+        mul("b",0)
+        tr(2)
+        ev(3)
+        mul("a",1)
+        q("b",0)
+        tr(3)
+        mul("b",1)
+        q("a",1)
+        mA(0,0)
+        mA(0,1)
+        mul("a",2)
+        q("b",1)
+        mB(0,0)
+        mB(1,0)
+        mB(0,1)
+        mB(1,1)
+        mul("a",3)
+        q("a",2)
+        q("a",3)
+        fin(0,0,"s",nc.sync)
+        fin(0,1,"s",nc.sync)
+        mA(1,0)
+        mA(1,1)
+        mul("b",2)
+        mul("b",3)
+        q("b",2)
+        q("b",3)
+        mB(2,0)
+        mB(3,0)
+        mB(2,1)
+        mB(3,1)
+        fin(1,0,"s",nc.scalar)
+        fin(1,1,"v",nc.sync)

@@ -53,11 +53,12 @@ def tile_mix_gradient_of_gated_sum_kernel(tc, g, wd_words, wd_scales, gs, zs, wa
         g_raw = {}
         fac = {}
 
-        def load_g(c, z):
-            t = sb.tile([P, PACK, TT], F32, name=f"g_raw{c}{z}", align_bytes=64)
-            src = g[z * 512 : (z + 1) * 512, c * TT : (c + 1) * TT]
+        def load_g(c, z, n=1):
+            t = sb.tile([P, PACK, n * TT], F32, name=f"g_raw{c}{z}", align_bytes=64)
+            src = g[z * 512 : (z + 1) * 512, c * TT : (c + n) * TT]
             nc.sync.dma_start(out=t[:], in_=src.rearrange("(p j) t -> p j t", j=PACK))
-            g_raw[c, z] = t
+            for i in range(n):
+                g_raw[c + i, z] = t[:, :, i * TT : (i + 1) * TT]
 
         def load_fac(key, c0, n):
             src = {"a": gs, "b": zs}[key]
@@ -80,37 +81,28 @@ def tile_mix_gradient_of_gated_sum_kernel(tc, g, wd_words, wd_scales, gs, zs, wa
             else:
                 nc.sync.dma_start(out=wb[:].bitcast(I32), in_=wb_words[0].bitcast(I32))
 
-        load_g(0,0)
-        load_g(0,1)
+        load_g(0,0,4)
+        load_g(0,1,2)
         load_w("d")
         load_scale("d",0,nc.sync)
         load_scale("d",1,nc.sync)
         load_scale("d",2,nc.sync)
         load_scale("d",3,nc.sync)
-        load_g(1,0)
-        load_g(1,1)
-        load_g(2,0)
-        load_g(2,1)
-        load_fac("a",0,1)
-        load_g(3,0)
-        load_g(3,1)
-        load_fac("b",0,1)
+        load_g(2,1,2)
+        load_fac("a",0,2)
         load_scale("a",0,nc.sync)
-        load_fac("a",1,1)
         load_scale("a",1,nc.sync)
-        load_fac("b",1,1)
         load_scale("a",2,nc.sync)
-        load_w("a")
         load_scale("a",3,nc.sync)
-        load_fac("a",2,1)
+        load_fac("b",0,2)
+        load_w("a")
         load_scale("b",0,nc.sync)
-        load_fac("a",3,1)
         load_scale("b",1,nc.sync)
-        load_w("b")
         load_scale("b",2,nc.sync)
-        load_fac("b",2,1)
         load_scale("b",3,nc.sync)
-        load_fac("b",3,1)
+        load_fac("a",2,2)
+        load_w("b")
+        load_fac("b",2,2)
 
         g_bf = [sb.tile([P, 2 * TT * PACK], BF16, name=f"g_bf{c}", align_bytes=64) for c in range(4)]
         g_q = [sb.tile([P, 2 * TT], U32, name=f"g_q{c}", align_bytes=64) for c in range(4)]
@@ -123,7 +115,7 @@ def tile_mix_gradient_of_gated_sum_kernel(tc, g, wd_words, wd_scales, gs, zs, wa
 
         def cast(c, z, eng):
             dst = g_bf[c][:, z * 512 : (z + 1) * 512].rearrange("p (c i j) -> p c j i", i=RUN, j=PACK)
-            src = g_raw[c, z][:].rearrange("p j (c i) -> p c j i", i=RUN)
+            src = g_raw[c, z].rearrange("p j (c i) -> p c j i", i=RUN)
             if eng == "v":
                 nc.vector.tensor_copy(out=dst, in_=src)
             else:
@@ -232,38 +224,44 @@ def tile_mix_gradient_of_gated_sum_kernel(tc, g, wd_words, wd_scales, gs, zs, wa
             queue.dma_start(out=dst, in_=res[:].rearrange("p (a t) -> p a t", a=2))
 
         cast(0,0,"v")
+        cast(2,0,"s")
+        cast(1,0,"v")
         qz(0,0)
-        cast(0,1,"v")
-        mz(0,0)
-        qz(0,1)
-        mz(0,1)
-        cast(1,0,"s")
-        cast(1,1,"v")
-        ev(0)
-        qg(1)
-        cast(2,0,"v")
-        tr(0)
-        m1(1)
-        cast(2,1,"v")
-        qg(2)
-        ev(1)
-        m1(2)
-        mul("a",0)
         cast(3,0,"s")
+        qz(1,0)
+        qz(2,0)
+        cast(0,1,"v")
+        cast(1,1,"s")
+        qz(3,0)
+        qz(0,1)
+        qz(1,1)
+        mz(0,0)
+        mz(0,1)
+        mz(1,0)
+        mz(1,1)
+        ev(0)
+        cast(2,1,"v")
         cast(3,1,"v")
+        qz(2,1)
+        tr(0)
+        qz(3,1)
+        ev(1)
+        mz(2,0)
+        mz(2,1)
         tr(1)
-        q("a",0)
-        qg(3)
+        mz(3,0)
+        mz(3,1)
         ev(2)
-        m1(3)
-        mul("b",0)
+        mul("a",0)
+        q("a",0)
+        mul("a",1)
         tr(2)
         ev(3)
-        mul("a",1)
-        q("b",0)
+        mul("b",0)
+        q("a",1)
         tr(3)
         mul("b",1)
-        q("a",1)
+        q("b",0)
         mA(0,0)
         mA(0,1)
         mul("a",2)
@@ -272,11 +270,11 @@ def tile_mix_gradient_of_gated_sum_kernel(tc, g, wd_words, wd_scales, gs, zs, wa
         mB(1,0)
         mB(0,1)
         mB(1,1)
+        fin(0,0,"s",nc.sync)
+        fin(0,1,"s",nc.sync)
         mul("a",3)
         q("a",2)
         q("a",3)
-        fin(0,0,"s",nc.sync)
-        fin(0,1,"s",nc.sync)
         mA(1,0)
         mA(1,1)
         mul("b",2)

@@ -19,7 +19,7 @@ MULT = mybir.AluOpType.mult
 P = 128
 PACK = 4
 TT = 128
-RUN = 4
+RUN = 2
 HALF = 256
 
 
@@ -42,10 +42,9 @@ def tile_mix_gradient_of_gated_sum_kernel(tc, g, wd_words, wd_scales, gs, zs, wa
         db_s = sb.tile([P, T], U8, name="db_s", align_bytes=64)
         ident = sb.tile([P, P], F32, name="ident", align_bytes=64)
 
-        nc.vector.memset(wd_s[:].bitcast(I32), 0)
+        nc.gpsimd.memset(wd_s[:].bitcast(I32), 0)
         nc.vector.memset(wa_s[:].bitcast(I32), 0)
         nc.vector.memset(wb_s[:].bitcast(I32), 0)
-        make_identity(nc, ident[:])
         for pad in range(3):
             nc.vector.memset(da_q[:, 2 * pad * HALF : (2 * pad + 1) * HALF], 0)
         nc.vector.memset(da_s[:].bitcast(I32), 0)
@@ -81,13 +80,14 @@ def tile_mix_gradient_of_gated_sum_kernel(tc, g, wd_words, wd_scales, gs, zs, wa
             else:
                 nc.sync.dma_start(out=wb[:].bitcast(I32), in_=wb_words[0].bitcast(I32))
 
-        load_g(0,0,4)
-        load_g(0,1,2)
+        load_scale("d",0,nc.gpsimd)
+        load_scale("d",1,nc.gpsimd)
+        load_scale("d",2,nc.gpsimd)
+        load_scale("d",3,nc.gpsimd)
+        load_g(0,0,2)
         load_w("d")
-        load_scale("d",0,nc.sync)
-        load_scale("d",1,nc.sync)
-        load_scale("d",2,nc.sync)
-        load_scale("d",3,nc.sync)
+        load_g(0,1,2)
+        load_g(2,0,2)
         load_g(2,1,2)
         load_fac("a",0,2)
         load_scale("a",0,nc.sync)
@@ -95,15 +95,17 @@ def tile_mix_gradient_of_gated_sum_kernel(tc, g, wd_words, wd_scales, gs, zs, wa
         load_scale("a",2,nc.sync)
         load_scale("a",3,nc.sync)
         load_fac("b",0,2)
+        load_fac("a",2,2)
         load_w("a")
         load_scale("b",0,nc.sync)
         load_scale("b",1,nc.sync)
         load_scale("b",2,nc.sync)
         load_scale("b",3,nc.sync)
-        load_fac("a",2,2)
         load_w("b")
-        load_fac("b",2,2)
+        load_fac("b",2,1)
+        load_fac("b",3,1)
 
+        make_identity(nc, ident[:])
         g_bf = [sb.tile([P, 2 * TT * PACK], BF16, name=f"g_bf{c}", align_bytes=64) for c in range(4)]
         g_q = [sb.tile([P, 2 * TT], U32, name=f"g_q{c}", align_bytes=64) for c in range(4)]
         g_s = [sb.tile([P, 2 * TT], U8, name=f"g_s{c}", align_bytes=64) for c in range(4)]
@@ -224,42 +226,42 @@ def tile_mix_gradient_of_gated_sum_kernel(tc, g, wd_words, wd_scales, gs, zs, wa
             queue.dma_start(out=dst, in_=res[:].rearrange("p (a t) -> p a t", a=2))
 
         cast(0,0,"v")
-        cast(2,0,"s")
         cast(1,0,"v")
         qz(0,0)
-        cast(3,0,"s")
         qz(1,0)
-        qz(2,0)
+        mz(0,0)
+        mz(1,0)
         cast(0,1,"v")
-        cast(1,1,"s")
-        qz(3,0)
+        cast(1,1,"v")
         qz(0,1)
         qz(1,1)
-        mz(0,0)
         mz(0,1)
-        mz(1,0)
         mz(1,1)
         ev(0)
+        ev(1)
+        cast(2,0,"v")
+        cast(3,0,"v")
+        qz(2,0)
+        qz(3,0)
+        mz(2,0)
+        mz(3,0)
+        tr(0)
         cast(2,1,"v")
         cast(3,1,"v")
         qz(2,1)
-        tr(0)
         qz(3,1)
-        ev(1)
-        mz(2,0)
-        mz(2,1)
         tr(1)
-        mz(3,0)
+        mz(2,1)
         mz(3,1)
         ev(2)
+        ev(3)
         mul("a",0)
-        q("a",0)
         mul("a",1)
         tr(2)
-        ev(3)
+        tr(3)
+        q("a",0)
         mul("b",0)
         q("a",1)
-        tr(3)
         mul("b",1)
         q("b",0)
         mA(0,0)
@@ -275,9 +277,9 @@ def tile_mix_gradient_of_gated_sum_kernel(tc, g, wd_words, wd_scales, gs, zs, wa
         mul("a",3)
         q("a",2)
         q("a",3)
+        mul("b",2)
         mA(1,0)
         mA(1,1)
-        mul("b",2)
         mul("b",3)
         q("b",2)
         q("b",3)

@@ -14,278 +14,251 @@ U8 = mybir.dt.uint8
 E4M3 = mybir.dt.float8_e4m3fn_x4
 E5M2 = mybir.dt.float8_e5m2_x4
 E2M1 = mybir.dt.float4_e2m1fn_x4
-MULT = mybir.AluOpType.mult
 
 P = 128
 PACK = 4
-TT = 128
+PASS = P * PACK
+PASSES = N // PASS
+BANK = 512
+TILE = P
+TILES = T // TILE
+HALF = T // 2
+FP4_BYTES = 2
+QUAD = 32
+SCALE_ROWS = 4
+ALIGN = 64
 RUN = 2
-HALF = 256
 
 
-def tile_mix_gradient_of_gated_sum_kernel(tc, g, wd_words, wd_scales, gs, zs, wa_words, wa_scales, wb_words, wb_scales, out):
+def cols(index, width):
+    return slice(index * width, (index + 1) * width)
+
+
+def by_row(ap):
+    return ap.rearrange("p j (c i) -> p c j i", i=RUN)
+
+
+def by_word(ap):
+    return ap.rearrange("p (c i j) -> p c j i", i=RUN, j=PACK)
+
+
+def tile_mix_gradient_of_gated_sum_kernel(
+    tc, g, wd_words, wd_scales, gs, zs, wa_words, wa_scales, wb_words, wb_scales, out
+):
     nc = tc.nc
     with ExitStack() as ctx:
-        sb = ctx.enter_context(tc.tile_pool(name="sb", bufs=1))
-        ps = ctx.enter_context(tc.psum_pool(name="ps", bufs=1))
+        sbuf = ctx.enter_context(tc.tile_pool(name="sbuf", bufs=1))
+        psum = ctx.enter_context(tc.psum_pool(name="psum", bufs=1))
         ctx.enter_context(tc.manual_schedule())
 
-        wd = sb.tile([P, 2 * 2 * R], U8, name="wd", align_bytes=64)
-        wa = sb.tile([P, K], U32, name="wa", align_bytes=64)
-        wb = sb.tile([P, 2 * K], U8, name="wb", align_bytes=64)
-        wd_s = sb.tile([P, 2 * R], U8, name="wd_s", align_bytes=64)
-        wa_s = sb.tile([P, K], U8, name="wa_s", align_bytes=64)
-        wb_s = sb.tile([P, K], U8, name="wb_s", align_bytes=64)
-        da_q = sb.tile([P, 5 * HALF], U32, name="da_q", align_bytes=64)
-        da_s = sb.tile([P, 5 * HALF], U8, name="da_s", align_bytes=64)
-        db_q = sb.tile([P, T], U32, name="db_q", align_bytes=64)
-        db_s = sb.tile([P, T], U8, name="db_s", align_bytes=64)
-        ident = sb.tile([P, P], F32, name="ident", align_bytes=64)
+        def sb(name, shape, dtype):
+            return sbuf.tile(shape, dtype, name=name, align_bytes=ALIGN)
 
-        nc.gpsimd.memset(wd_s[:].bitcast(I32), 0)
-        nc.vector.memset(wa_s[:].bitcast(I32), 0)
-        nc.vector.memset(wb_s[:].bitcast(I32), 0)
-        for pad in range(3):
-            nc.vector.memset(da_q[:, 2 * pad * HALF : (2 * pad + 1) * HALF], 0)
-        nc.vector.memset(da_s[:].bitcast(I32), 0)
+        def bank(name, index):
+            return psum.tile([P, BANK], F32, name=name, tag=f"bank{index}")
 
-        g_raw = {}
-        fac = {}
+        wd = sb("wd", [P, PASSES * R * FP4_BYTES], U8)
+        wa = sb("wa", [P, K], U32)
+        wb = sb("wb", [P, K * FP4_BYTES], U8)
+        wd_scale = sb("wd_scale", [P, PASSES * R], U8)
+        wa_scale = sb("wa_scale", [P, K], U8)
+        wb_scale = sb("wb_scale", [P, K], U8)
+        da_codes = sb("da_codes", [P, 4 * HALF], U32)
+        da_scale = sb("da_scale", [P, 4 * HALF], U8)
+        db_codes = sb("db_codes", [P, T], U32)
+        db_scale = sb("db_scale", [P, T], U8)
+        identity = sb("identity", [P, P], F32)
 
-        def load_g(c, z, n=1):
-            t = sb.tile([P, PACK, n * TT], F32, name=f"g_raw{c}{z}", align_bytes=64)
-            src = g[z * 512 : (z + 1) * 512, c * TT : (c + n) * TT]
-            nc.sync.dma_start(out=t[:], in_=src.rearrange("(p j) t -> p j t", j=PACK))
-            for i in range(n):
-                g_raw[c + i, z] = t[:, :, i * TT : (i + 1) * TT]
+        for scale in (wd_scale, wa_scale, wb_scale):
+            nc.vector.memset(scale[:].bitcast(I32), 0)
+        make_identity(nc, identity[:])
+        for half in range(2):
+            nc.vector.memset(da_codes[:, cols(2 * half, HALF)], 0)
+            nc.vector.memset(da_scale[:, cols(2 * half, HALF)].bitcast(I32), 0)
 
-        def load_fac(key, c0, n):
-            src = {"a": gs, "b": zs}[key]
-            t = sb.tile([P, PACK, n * TT], F32, name=f"fac{key}{c0}", align_bytes=64)
-            nc.sync.dma_start(out=t[:], in_=src[:, c0 * TT : (c0 + n) * TT].rearrange("(p j) t -> p j t", j=PACK))
-            for i in range(n):
-                fac[key, c0 + i] = t[:, :, i * TT : (i + 1) * TT]
+        def load_rows(name, rows, first_tile, tiles):
+            raw = sb(name, [P, PACK, tiles * TILE], F32)
+            tokens = slice(first_tile * TILE, (first_tile + tiles) * TILE)
+            nc.sync.dma_start(out=raw[:], in_=rows[:, tokens].rearrange("(p j) t -> p j t", j=PACK))
+            return [raw[:, :, cols(i, TILE)] for i in range(tiles)]
 
-        def load_scale(key, r, eng):
-            plane, src = {"d": (wd_s, wd_scales), "a": (wa_s, wa_scales), "b": (wb_s, wb_scales)}[key]
-            z = src.shape[0]
-            dst = plane[:].bitcast(I32)[r:P:32, :].rearrange("q (z n) -> q z n", z=z)
-            eng.dma_start(out=dst, in_=src.bitcast(I32).rearrange("z (q r) n -> r q z n", r=4)[r])
+        def load_words(words, source):
+            passes = source.shape[0]
+            nc.sync.dma_start(
+                out=words[:].bitcast(I32).rearrange("p (z c) -> p z c", z=passes),
+                in_=source.bitcast(I32).rearrange("z p c -> p z c"),
+            )
 
-        def load_w(key):
-            if key == "d":
-                nc.sync.dma_start(out=wd[:].bitcast(I32).rearrange("p (z n) -> p z n", z=2), in_=wd_words.bitcast(I32).rearrange("z p n -> p z n"))
-            elif key == "a":
-                nc.sync.dma_start(out=wa[:].bitcast(I32), in_=wa_words[0].rearrange("p n j -> p (n j)").bitcast(I32))
-            else:
-                nc.sync.dma_start(out=wb[:].bitcast(I32), in_=wb_words[0].bitcast(I32))
+        def load_scales(scale, source):
+            passes = source.shape[0]
+            rows = source.bitcast(I32).rearrange("z (q s) c -> s q z c", s=SCALE_ROWS)
+            for s in range(SCALE_ROWS):
+                nc.sync.dma_start(
+                    out=scale[:].bitcast(I32)[s:P:QUAD, :].rearrange("q (z c) -> q z c", z=passes),
+                    in_=rows[s],
+                )
 
-        load_scale("d",0,nc.gpsimd)
-        load_scale("d",1,nc.gpsimd)
-        load_scale("d",2,nc.gpsimd)
-        load_scale("d",3,nc.gpsimd)
-        load_g(0,0,2)
-        load_w("d")
-        load_g(0,1,2)
-        load_g(2,0,2)
-        load_g(2,1,2)
-        load_fac("a",0,2)
-        load_scale("a",0,nc.sync)
-        load_scale("a",1,nc.sync)
-        load_scale("a",2,nc.sync)
-        load_scale("a",3,nc.sync)
-        load_fac("b",0,2)
-        load_fac("a",2,2)
-        load_w("a")
-        load_scale("b",0,nc.sync)
-        load_scale("b",1,nc.sync)
-        load_scale("b",2,nc.sync)
-        load_scale("b",3,nc.sync)
-        load_w("b")
-        load_fac("b",2,1)
-        load_fac("b",3,1)
+        g_first = [load_rows("g_00", g[cols(0, PASS), :], 0, 2)]
+        load_words(wd, wd_words)
+        load_scales(wd_scale, wd_scales)
+        g_first.append(load_rows("g_01", g[cols(1, PASS), :], 0, 2))
+        g_second = [load_rows(f"g_1{z}", g[cols(z, PASS), :], 2, 2) for z in range(PASSES)]
+        g_raw = [g_first[z] + g_second[z] for z in range(PASSES)]
+        gs_raw = load_rows("gs_0", gs, 0, 2)
+        load_scales(wa_scale, wa_scales)
+        zs_raw = load_rows("zs_0", zs, 0, 2)
+        gs_raw = gs_raw + load_rows("gs_1", gs, 2, 2)
+        load_words(wa, wa_words.rearrange("z p c j -> z p (c j)"))
+        load_scales(wb_scale, wb_scales)
+        load_words(wb, wb_words)
+        zs_raw = zs_raw + load_rows("zs_2", zs, 2, 1) + load_rows("zs_3", zs, 3, 1)
 
-        make_identity(nc, ident[:])
-        g_bf = [sb.tile([P, 2 * TT * PACK], BF16, name=f"g_bf{c}", align_bytes=64) for c in range(4)]
-        g_q = [sb.tile([P, 2 * TT], U32, name=f"g_q{c}", align_bytes=64) for c in range(4)]
-        g_s = [sb.tile([P, 2 * TT], U8, name=f"g_s{c}", align_bytes=64) for c in range(4)]
-        dT_ps = {}
-        dT_sb = {}
-        d_ps = {}
-        prod = {}
-        o_ps = {}
+        g_codes = {}
+        g_scale = {}
+        dt_psum = {}
+        dt_sbuf = {}
+        d_psum = {}
 
-        def cast(c, z, eng):
-            dst = g_bf[c][:, z * 512 : (z + 1) * 512].rearrange("p (c i j) -> p c j i", i=RUN, j=PACK)
-            src = g_raw[c, z].rearrange("p j (c i) -> p c j i", i=RUN)
-            if eng == "v":
-                nc.vector.tensor_copy(out=dst, in_=src)
-            else:
-                nc.scalar.copy(out=dst, in_=src)
+        def quantise_g(half, z):
+            tiles = (2 * half, 2 * half + 1)
+            rounded = {}
+            for c in tiles:
+                rounded[c] = sb(f"g_bf16_{c}{z}", [P, TILE * PACK], BF16)
+                nc.vector.tensor_copy(out=by_word(rounded[c][:]), in_=by_row(g_raw[z][c]))
+            for c in tiles:
+                g_codes[c, z] = sb(f"g_codes_{c}{z}", [P, TILE], U32)
+                g_scale[c, z] = sb(f"g_scale_{c}{z}", [P, TILE], U8)
+                nc.vector.quantize_mx(out=g_codes[c, z][:].bitcast(E5M2), scales=g_scale[c, z][:], in_=rounded[c][:])
 
-        def qg(c):
-            nc.vector.quantize_mx(out=g_q[c][:].bitcast(E5M2), scales=g_s[c][:], in_=g_bf[c][:])
-
-        def qz(c, z):
-            nc.vector.quantize_mx(out=g_q[c][:, z * TT : (z + 1) * TT].bitcast(E5M2), scales=g_s[c][:, z * TT : (z + 1) * TT], in_=g_bf[c][:, z * 512 : (z + 1) * 512])
-
-        def mz(c, z):
+        def first_product(c, z):
             if z == 0:
-                dT_ps[c] = ps.tile([P, R], F32, name=f"dT{c}", tag=f"bank{c}")
+                dt_psum[c] = bank(f"dt_{c}", c)
             nc.tensor.matmul_mx(
-                out=dT_ps[c][:],
-                lhsT=g_q[c][:, z * TT : (z + 1) * TT].bitcast(E5M2),
-                lhsT_scale=g_s[c][:, z * TT : (z + 1) * TT],
-                rhs=wd[:, z * 2 * R : (z + 1) * 2 * R].bitcast(E2M1),
-                rhs_scale=wd_s[:, z * R : (z + 1) * R],
+                out=dt_psum[c][:],
+                lhsT=g_codes[c, z][:].bitcast(E5M2),
+                lhsT_scale=g_scale[c, z][:],
+                rhs=wd[:, cols(z, R * FP4_BYTES)].bitcast(E2M1),
+                rhs_scale=wd_scale[:, cols(z, R)],
                 start=(z == 0),
-                stop=(z == 1),
+                stop=(z == PASSES - 1),
             )
 
-        def m1(c):
-            acc = ps.tile([P, R], F32, name=f"dT{c}", tag=f"bank{c}")
-            for z in range(2):
-                nc.tensor.matmul_mx(
-                    out=acc[:],
-                    lhsT=g_q[c][:, z * TT : (z + 1) * TT].bitcast(E5M2),
-                    lhsT_scale=g_s[c][:, z * TT : (z + 1) * TT],
-                    rhs=wd[:, z * 2 * R : (z + 1) * 2 * R].bitcast(E2M1),
-                    rhs_scale=wd_s[:, z * R : (z + 1) * R],
-                    start=(z == 0),
-                    stop=(z == 1),
-                )
-            dT_ps[c] = acc
+        def copy_out_dt(c):
+            dt_sbuf[c] = sb(f"dt_sbuf_{c}", [P, PACK, P], F32)
+            nc.scalar.copy(out=dt_sbuf[c][:], in_=dt_psum[c][:].rearrange("t (m j) -> t j m", j=PACK))
 
-        def ev(c):
-            t = sb.tile([P, PACK, P], F32, name=f"dT_sb{c}", align_bytes=64)
-            nc.scalar.copy(out=t[:], in_=dT_ps[c][:].rearrange("t (m j) -> t j m", j=PACK))
-            dT_sb[c] = t
-
-        def tr(c):
-            acc = ps.tile([P, PACK, TT], F32, name=f"d{c}", tag=f"d{c}")
+        def transpose_dt(c):
+            d_psum[c] = bank(f"d_{c}", TILES + c)
             for j in range(PACK):
-                nc.tensor.transpose(acc[:, j, :], dT_sb[c][:, j, :], ident[:])
-            d_ps[c] = acc
+                nc.tensor.transpose(d_psum[c][:, cols(j, TILE)], dt_sbuf[c][:, j, :], identity[:])
 
-        def mul(key, c):
-            t = sb.tile([P, TT * PACK], BF16, name=f"prod{key}{c}", align_bytes=64)
+        for z in range(PASSES):
+            quantise_g(0, z)
+            first_product(0, z)
+            first_product(1, z)
+        copy_out_dt(0)
+        copy_out_dt(1)
+        quantise_g(1, 0)
+        for c in (0, 1):
+            first_product(2 + c, 0)
+            transpose_dt(c)
+        quantise_g(1, 1)
+        first_product(2, 1)
+        first_product(3, 1)
+        copy_out_dt(2)
+        copy_out_dt(3)
+
+        def multiply(name, factor, c):
+            product = sb(f"{name}_bf16_{c}", [P, TILE * PACK], BF16)
             nc.vector.tensor_tensor(
-                out=t[:].rearrange("p (c i j) -> p c j i", i=RUN, j=PACK),
-                in0=d_ps[c][:].rearrange("p j (c i) -> p c j i", i=RUN),
-                in1=fac[key, c].rearrange("p j (c i) -> p c j i", i=RUN),
-                op=MULT,
+                out=by_word(product[:]),
+                in0=by_row(d_psum[c][:].rearrange("p (j t) -> p j t", j=PACK)),
+                in1=by_row(factor[c]),
+                op=mybir.AluOpType.mult,
             )
-            prod[key, c] = t
+            return product
 
-        def q(key, c):
-            if key == "a":
-                c0 = (2 * (c // 2) + 1) * HALF + (c % 2) * TT
-                nc.vector.quantize_mx(out=da_q[:, c0 : c0 + TT].bitcast(E5M2), scales=da_s[:, c0 : c0 + TT], in_=prod[key, c][:])
+        def quantise_da(product, c):
+            first = (2 * (c // 2) + 1) * HALF + (c % 2) * TILE
+            where = slice(first, first + TILE)
+            nc.vector.quantize_mx(out=da_codes[:, where].bitcast(E5M2), scales=da_scale[:, where], in_=product[:])
+
+        def quantise_db(product, c):
+            where = cols(c, TILE)
+            nc.vector.quantize_mx(out=db_codes[:, where].bitcast(E4M3), scales=db_scale[:, where], in_=product[:])
+
+        def product_a(acc, side, half, kt, start):
+            first = (2 * half + 1 - side) * HALF
+            window = slice(first, first + BANK)
+            nc.tensor.matmul_mx(
+                out=acc[:],
+                lhsT=wa[:, cols(kt, P)].bitcast(E4M3),
+                lhsT_scale=wa_scale[:, cols(kt, P)],
+                rhs=da_codes[:, window].bitcast(E5M2),
+                rhs_scale=da_scale[:, window],
+                start=start,
+                stop=False,
+            )
+
+        def product_b(acc, side, c, kt, stop):
+            first = side * HALF + (c % 2) * TILE
+            nc.tensor.matmul_mx(
+                out=acc[:, first : first + TILE],
+                lhsT=wb[:, cols(kt, P * FP4_BYTES)].bitcast(E2M1),
+                lhsT_scale=wb_scale[:, cols(kt, P)],
+                rhs=db_codes[:, cols(c, TILE)].bitcast(E4M3),
+                rhs_scale=db_scale[:, cols(c, TILE)],
+                start=False,
+                stop=stop,
+            )
+
+        out_rows = out.rearrange("(kt p) t -> p kt t", p=P)
+
+        da_0 = multiply("da", gs_raw, 0)
+        da_1 = multiply("da", gs_raw, 1)
+        transpose_dt(2)
+        transpose_dt(3)
+        quantise_da(da_0, 0)
+        db_0 = multiply("db", zs_raw, 0)
+        quantise_da(da_1, 1)
+
+        first_sums = [bank(f"first_sum_{b}", b) for b in range(2)]
+        for b in range(2):
+            for side in range(2):
+                product_a(first_sums[b], side, 0, 2 * b + side, start=(side == 0))
+        db_1 = multiply("db", zs_raw, 1)
+        quantise_db(db_0, 0)
+        da_2 = multiply("da", gs_raw, 2)
+        quantise_db(db_1, 1)
+        for b in range(2):
+            for c in (0, 1):
+                for side in range(2):
+                    product_b(first_sums[b], side, c, 2 * b + side, stop=(c == 1 and side == 1))
+        for b in range(2):
+            result = sb(f"first_result_{b}", [P, BANK], F32)
+            nc.scalar.copy(out=result[:], in_=first_sums[b][:])
+            nc.sync.dma_start(
+                out=out_rows[:, cols(b, 2), cols(0, HALF)], in_=result[:].rearrange("p (kt t) -> p kt t", kt=2)
+            )
+
+        da_3 = multiply("da", gs_raw, 3)
+        quantise_da(da_2, 2)
+        quantise_da(da_3, 3)
+        db_2 = multiply("db", zs_raw, 2)
+
+        second_sums = [bank(f"second_sum_{kt}", 2 + kt) for kt in range(K // P)]
+        for kt, acc in enumerate(second_sums):
+            product_a(acc, 1, 1, kt, start=True)
+        db_3 = multiply("db", zs_raw, 3)
+        quantise_db(db_2, 2)
+        quantise_db(db_3, 3)
+        for kt, acc in enumerate(second_sums):
+            product_b(acc, 1, 2, kt, stop=False)
+            product_b(acc, 1, 3, kt, stop=True)
+        for kt, acc in enumerate(second_sums):
+            result = sb(f"second_result_{kt}", [P, HALF], F32)
+            if kt % 2 == 0:
+                nc.scalar.copy(out=result[:], in_=acc[:, cols(1, HALF)])
             else:
-                c0 = c * TT
-                nc.vector.quantize_mx(out=db_q[:, c0 : c0 + TT].bitcast(E4M3), scales=db_s[:, c0 : c0 + TT], in_=prod[key, c][:])
-
-        def mA(h, b):
-            acc = ps.tile([P, 2 * HALF], F32, name=f"o{h}{b}", tag=f"bank{2 * h + b}")
-            o_ps[h, b] = acc
-            for a in range(2):
-                kt = 2 * b + a
-                w0 = (2 * h + 1 - a) * HALF
-                nc.tensor.matmul_mx(
-                    out=acc[:],
-                    lhsT=wa[:, kt * P : (kt + 1) * P].bitcast(E4M3),
-                    lhsT_scale=wa_s[:, kt * P : (kt + 1) * P],
-                    rhs=da_q[:, w0 : w0 + 2 * HALF].bitcast(E5M2),
-                    rhs_scale=da_s[:, w0 : w0 + 2 * HALF],
-                    start=(a == 0),
-                    stop=False,
-                )
-
-        def mB(c, b):
-            h = c // 2
-            for a in range(2):
-                kt = 2 * b + a
-                c0 = a * HALF + (c % 2) * TT
-                nc.tensor.matmul_mx(
-                    out=o_ps[h, b][:, c0 : c0 + TT],
-                    lhsT=wb[:, kt * 2 * P : (kt + 1) * 2 * P].bitcast(E2M1),
-                    lhsT_scale=wb_s[:, kt * P : (kt + 1) * P],
-                    rhs=db_q[:, c * TT : (c + 1) * TT].bitcast(E4M3),
-                    rhs_scale=db_s[:, c * TT : (c + 1) * TT],
-                    start=False,
-                    stop=(c % 2 == 1 and a == 1),
-                )
-
-        def fin(h, b, eng, queue):
-            res = sb.tile([P, 2 * HALF], F32, name=f"res{h}{b}", align_bytes=64)
-            if eng == "v":
-                nc.vector.tensor_copy(out=res[:], in_=o_ps[h, b][:])
-            else:
-                nc.scalar.copy(out=res[:], in_=o_ps[h, b][:])
-            dst = out.rearrange("(a p) t -> p a t", p=P)[:, 2 * b : 2 * b + 2, h * HALF : (h + 1) * HALF]
-            queue.dma_start(out=dst, in_=res[:].rearrange("p (a t) -> p a t", a=2))
-
-        cast(0,0,"v")
-        cast(1,0,"v")
-        qz(0,0)
-        qz(1,0)
-        mz(0,0)
-        mz(1,0)
-        cast(0,1,"v")
-        cast(1,1,"v")
-        qz(0,1)
-        qz(1,1)
-        mz(0,1)
-        mz(1,1)
-        ev(0)
-        ev(1)
-        cast(2,0,"v")
-        cast(3,0,"v")
-        qz(2,0)
-        qz(3,0)
-        mz(2,0)
-        mz(3,0)
-        tr(0)
-        cast(2,1,"v")
-        cast(3,1,"v")
-        qz(2,1)
-        qz(3,1)
-        tr(1)
-        mz(2,1)
-        mz(3,1)
-        ev(2)
-        ev(3)
-        mul("a",0)
-        mul("a",1)
-        tr(2)
-        tr(3)
-        q("a",0)
-        mul("b",0)
-        q("a",1)
-        mul("b",1)
-        q("b",0)
-        mA(0,0)
-        mA(0,1)
-        mul("a",2)
-        q("b",1)
-        mB(0,0)
-        mB(1,0)
-        mB(0,1)
-        mB(1,1)
-        fin(0,0,"s",nc.sync)
-        fin(0,1,"s",nc.sync)
-        mul("a",3)
-        q("a",2)
-        q("a",3)
-        mul("b",2)
-        mA(1,0)
-        mA(1,1)
-        mul("b",3)
-        q("b",2)
-        q("b",3)
-        mB(2,0)
-        mB(3,0)
-        mB(2,1)
-        mB(3,1)
-        fin(1,0,"s",nc.scalar)
-        fin(1,1,"v",nc.sync)
+                nc.vector.tensor_copy(out=result[:], in_=acc[:, cols(1, HALF)])
+            nc.sync.dma_start(out=out_rows[:, kt, cols(1, HALF)], in_=result[:])

@@ -27,7 +27,7 @@ FP4_BYTES = 2
 QUAD = 32
 SCALE_ROWS = 4
 ALIGN = 64
-RUN = 2
+RUN = 4
 
 
 def cols(index, width):
@@ -83,11 +83,7 @@ def tile_mix_gradient_of_gated_sum_kernel(
             return [raw[:, :, cols(i, TILE)] for i in range(tiles)]
 
         def load_words(words, source):
-            passes = source.shape[0]
-            nc.sync.dma_start(
-                out=words[:].bitcast(I32).rearrange("p (z c) -> p z c", z=passes),
-                in_=source.bitcast(I32).rearrange("z p c -> p z c"),
-            )
+            nc.sync.dma_start(out=words.bitcast(I32), in_=source.bitcast(I32))
 
         def load_scales(scale, source):
             passes = source.shape[0]
@@ -98,19 +94,19 @@ def tile_mix_gradient_of_gated_sum_kernel(
                     in_=rows[s],
                 )
 
-        g_first = [load_rows("g_00", g[cols(0, PASS), :], 0, 2)]
-        load_words(wd, wd_words)
+        g_raw = [load_rows("g_0", g[cols(0, PASS), :], 0, TILES)]
+        load_words(wd[:, cols(0, R * FP4_BYTES)], wd_words[0])
         load_scales(wd_scale, wd_scales)
-        g_first.append(load_rows("g_01", g[cols(1, PASS), :], 0, 2))
-        g_second = [load_rows(f"g_1{z}", g[cols(z, PASS), :], 2, 2) for z in range(PASSES)]
-        g_raw = [g_first[z] + g_second[z] for z in range(PASSES)]
+        g_first_half = load_rows("g_10", g[cols(1, PASS), :], 0, 2)
+        load_words(wd[:, cols(1, R * FP4_BYTES)], wd_words[1])
+        g_raw.append(g_first_half + load_rows("g_11", g[cols(1, PASS), :], 2, 2))
         gs_raw = load_rows("gs_0", gs, 0, 2)
-        load_scales(wa_scale, wa_scales)
         zs_raw = load_rows("zs_0", zs, 0, 2)
+        load_scales(wa_scale, wa_scales)
+        load_words(wa[:], wa_words[0].rearrange("p c j -> p (c j)"))
         gs_raw = gs_raw + load_rows("gs_1", gs, 2, 2)
-        load_words(wa, wa_words.rearrange("z p c j -> z p (c j)"))
         load_scales(wb_scale, wb_scales)
-        load_words(wb, wb_words)
+        load_words(wb[:], wb_words[0])
         zs_raw = zs_raw + load_rows("zs_2", zs, 2, 1) + load_rows("zs_3", zs, 3, 1)
 
         g_codes = {}
@@ -119,12 +115,14 @@ def tile_mix_gradient_of_gated_sum_kernel(
         dt_sbuf = {}
         d_psum = {}
 
-        def quantise_g(half, z):
-            tiles = (2 * half, 2 * half + 1)
+        def quantise_g(tiles, z, scalar_helps):
             rounded = {}
             for c in tiles:
                 rounded[c] = sb(f"g_bf16_{c}{z}", [P, TILE * PACK], BF16)
-                nc.vector.tensor_copy(out=by_word(rounded[c][:]), in_=by_row(g_raw[z][c]))
+                if scalar_helps and c % 2 == 1:
+                    nc.scalar.copy(out=by_word(rounded[c][:]), in_=by_row(g_raw[z][c]))
+                else:
+                    nc.vector.tensor_copy(out=by_word(rounded[c][:]), in_=by_row(g_raw[z][c]))
             for c in tiles:
                 g_codes[c, z] = sb(f"g_codes_{c}{z}", [P, TILE], U32)
                 g_scale[c, z] = sb(f"g_scale_{c}{z}", [P, TILE], U8)
@@ -152,40 +150,48 @@ def tile_mix_gradient_of_gated_sum_kernel(
             for j in range(PACK):
                 nc.tensor.transpose(d_psum[c][:, cols(j, TILE)], dt_sbuf[c][:, j, :], identity[:])
 
-        for z in range(PASSES):
-            quantise_g(0, z)
-            first_product(0, z)
-            first_product(1, z)
+        quantise_g(range(TILES), 0, scalar_helps=True)
+        for c in range(TILES - 1):
+            first_product(c, 0)
+        quantise_g((0, 1), 1, scalar_helps=True)
+        first_product(0, 1)
+        first_product(1, 1)
+        first_product(TILES - 1, 0)
         copy_out_dt(0)
         copy_out_dt(1)
-        quantise_g(1, 0)
-        for c in (0, 1):
-            first_product(2 + c, 0)
-            transpose_dt(c)
-        quantise_g(1, 1)
+        quantise_g((2, 3), 1, scalar_helps=False)
+        transpose_dt(0)
+        transpose_dt(1)
         first_product(2, 1)
         first_product(3, 1)
         copy_out_dt(2)
         copy_out_dt(3)
 
-        def multiply(name, factor, c):
-            product = sb(f"{name}_bf16_{c}", [P, TILE * PACK], BF16)
+        da_bf16 = sb("da_bf16", [P, T * PACK], BF16)
+        db_bf16 = sb("db_bf16", [P, T * PACK], BF16)
+
+        def multiply(product, factor, c):
             nc.vector.tensor_tensor(
-                out=by_word(product[:]),
+                out=by_word(product[:, cols(c, TILE * PACK)]),
                 in0=by_row(d_psum[c][:].rearrange("p (j t) -> p j t", j=PACK)),
                 in1=by_row(factor[c]),
                 op=mybir.AluOpType.mult,
             )
-            return product
 
-        def quantise_da(product, c):
-            first = (2 * (c // 2) + 1) * HALF + (c % 2) * TILE
-            where = slice(first, first + TILE)
-            nc.vector.quantize_mx(out=da_codes[:, where].bitcast(E5M2), scales=da_scale[:, where], in_=product[:])
+        def quantise_da(first_token, tokens):
+            first = first_token + (first_token // HALF + 1) * HALF
+            nc.vector.quantize_mx(
+                out=da_codes[:, first : first + tokens].bitcast(E5M2),
+                scales=da_scale[:, first : first + tokens],
+                in_=da_bf16[:, first_token * PACK : (first_token + tokens) * PACK],
+            )
 
-        def quantise_db(product, c):
-            where = cols(c, TILE)
-            nc.vector.quantize_mx(out=db_codes[:, where].bitcast(E4M3), scales=db_scale[:, where], in_=product[:])
+        def quantise_db(first_token, tokens):
+            nc.vector.quantize_mx(
+                out=db_codes[:, first_token : first_token + tokens].bitcast(E4M3),
+                scales=db_scale[:, first_token : first_token + tokens],
+                in_=db_bf16[:, first_token * PACK : (first_token + tokens) * PACK],
+            )
 
         def product_a(acc, side, half, kt, start):
             first = (2 * half + 1 - side) * HALF
@@ -214,22 +220,19 @@ def tile_mix_gradient_of_gated_sum_kernel(
 
         out_rows = out.rearrange("(kt p) t -> p kt t", p=P)
 
-        da_0 = multiply("da", gs_raw, 0)
-        da_1 = multiply("da", gs_raw, 1)
+        multiply(da_bf16, gs_raw, 0)
+        multiply(da_bf16, gs_raw, 1)
         transpose_dt(2)
         transpose_dt(3)
-        quantise_da(da_0, 0)
-        db_0 = multiply("db", zs_raw, 0)
-        quantise_da(da_1, 1)
+        multiply(db_bf16, zs_raw, 0)
+        multiply(db_bf16, zs_raw, 1)
+        quantise_da(0, HALF)
+        quantise_db(0, HALF)
 
         first_sums = [bank(f"first_sum_{b}", b) for b in range(2)]
         for b in range(2):
             for side in range(2):
                 product_a(first_sums[b], side, 0, 2 * b + side, start=(side == 0))
-        db_1 = multiply("db", zs_raw, 1)
-        quantise_db(db_0, 0)
-        da_2 = multiply("da", gs_raw, 2)
-        quantise_db(db_1, 1)
         for b in range(2):
             for c in (0, 1):
                 for side in range(2):
@@ -241,17 +244,18 @@ def tile_mix_gradient_of_gated_sum_kernel(
                 out=out_rows[:, cols(b, 2), cols(0, HALF)], in_=result[:].rearrange("p (kt t) -> p kt t", kt=2)
             )
 
-        da_3 = multiply("da", gs_raw, 3)
-        quantise_da(da_2, 2)
-        quantise_da(da_3, 3)
-        db_2 = multiply("db", zs_raw, 2)
+        multiply(da_bf16, gs_raw, 2)
+        multiply(da_bf16, gs_raw, 3)
+        quantise_da(2 * TILE, TILE)
+        quantise_da(3 * TILE, TILE)
+        multiply(db_bf16, zs_raw, 2)
 
         second_sums = [bank(f"second_sum_{kt}", 2 + kt) for kt in range(K // P)]
         for kt, acc in enumerate(second_sums):
             product_a(acc, 1, 1, kt, start=True)
-        db_3 = multiply("db", zs_raw, 3)
-        quantise_db(db_2, 2)
-        quantise_db(db_3, 3)
+        multiply(db_bf16, zs_raw, 3)
+        quantise_db(2 * TILE, TILE)
+        quantise_db(3 * TILE, TILE)
         for kt, acc in enumerate(second_sums):
             product_b(acc, 1, 2, kt, stop=False)
             product_b(acc, 1, 3, kt, stop=True)

from contextlib import ExitStack

import concourse.mybir as mybir
from concourse.masks import make_identity

N, R, K, T = 1024, 512, 512, 512
FLOPS = 2 * N * R * T + 2 * 2 * R * K * T

F32 = mybir.dt.float32
BF16 = mybir.dt.bfloat16
I32 = mybir.dt.int32
U32 = mybir.dt.uint32
U8 = mybir.dt.uint8
E4M3 = mybir.dt.float8_e4m3fn_x4
E5M2 = mybir.dt.float8_e5m2_x4
E2M1 = mybir.dt.float4_e2m1fn_x4

P = 128
PACK = 4
PASS = P * PACK
PASSES = N // PASS
BANK = 512
TILE = P
TILES = T // TILE
HALF = T // 2
FP4_BYTES = 2
QUAD = 32
SCALE_ROWS = 4
ALIGN = 64
RUN = 4


def cols(index, width):
    return slice(index * width, (index + 1) * width)


def by_row(ap):
    return ap.rearrange("p j (c i) -> p c j i", i=RUN)


def by_word(ap):
    return ap.rearrange("p (c i j) -> p c j i", i=RUN, j=PACK)


def tile_mix_gradient_of_gated_sum_kernel(
    tc, g, wd_words, wd_scales, gs, zs, wa_words, wa_scales, wb_words, wb_scales, out
):
    nc = tc.nc
    with ExitStack() as ctx:
        sbuf = ctx.enter_context(tc.tile_pool(name="sbuf", bufs=1))
        psum = ctx.enter_context(tc.psum_pool(name="psum", bufs=1))
        ctx.enter_context(tc.manual_schedule())

        def sb(name, shape, dtype):
            return sbuf.tile(shape, dtype, name=name, align_bytes=ALIGN)

        def bank(name, index):
            return psum.tile([P, BANK], F32, name=name, tag=f"bank{index}")

        wd = sb("wd", [P, PASSES * R * FP4_BYTES], U8)
        wa = sb("wa", [P, K], U32)
        wb = sb("wb", [P, K * FP4_BYTES], U8)
        wd_scale = sb("wd_scale", [P, PASSES * R], U8)
        wa_scale = sb("wa_scale", [P, K], U8)
        wb_scale = sb("wb_scale", [P, K], U8)
        da_codes = sb("da_codes", [P, 4 * HALF], U32)
        da_scale = sb("da_scale", [P, 4 * HALF], U8)
        db_codes = sb("db_codes", [P, T], U32)
        db_scale = sb("db_scale", [P, T], U8)
        identity = sb("identity", [P, P], F32)

        for scale in (wd_scale, wa_scale, wb_scale):
            nc.vector.memset(scale[:].bitcast(I32), 0)
        make_identity(nc, identity[:])
        for half in range(2):
            nc.vector.memset(da_codes[:, cols(2 * half, HALF)], 0)
            nc.vector.memset(da_scale[:, cols(2 * half, HALF)].bitcast(I32), 0)

        def load_rows(name, rows, first_tile, tiles):
            raw = sb(name, [P, PACK, tiles * TILE], F32)
            tokens = slice(first_tile * TILE, (first_tile + tiles) * TILE)
            nc.sync.dma_start(out=raw[:], in_=rows[:, tokens].rearrange("(p j) t -> p j t", j=PACK))
            return [raw[:, :, cols(i, TILE)] for i in range(tiles)]

        def load_words(words, source):
            nc.sync.dma_start(out=words.bitcast(I32), in_=source.bitcast(I32))

        def load_scales(scale, source):
            passes = source.shape[0]
            rows = source.bitcast(I32).rearrange("z (q s) c -> s q z c", s=SCALE_ROWS)
            for s in range(SCALE_ROWS):
                nc.sync.dma_start(
                    out=scale[:].bitcast(I32)[s:P:QUAD, :].rearrange("q (z c) -> q z c", z=passes),
                    in_=rows[s],
                )

        g_raw = [load_rows("g_0", g[cols(0, PASS), :], 0, TILES)]
        load_words(wd[:, cols(0, R * FP4_BYTES)], wd_words[0])
        load_scales(wd_scale, wd_scales)
        g_first_half = load_rows("g_10", g[cols(1, PASS), :], 0, 2)
        load_words(wd[:, cols(1, R * FP4_BYTES)], wd_words[1])
        g_raw.append(g_first_half + load_rows("g_11", g[cols(1, PASS), :], 2, 2))
        gs_raw = load_rows("gs_0", gs, 0, 2)
        zs_raw = load_rows("zs_0", zs, 0, 2)
        load_scales(wa_scale, wa_scales)
        load_words(wa[:], wa_words[0].rearrange("p c j -> p (c j)"))
        gs_raw = gs_raw + load_rows("gs_1", gs, 2, 2)
        load_scales(wb_scale, wb_scales)
        load_words(wb[:], wb_words[0])
        zs_raw = zs_raw + load_rows("zs_2", zs, 2, 1) + load_rows("zs_3", zs, 3, 1)

        g_codes = {}
        g_scale = {}
        dt_psum = {}
        dt_sbuf = {}
        d_psum = {}

        def quantise_g(tiles, z, scalar_helps):
            rounded = {}
            for c in tiles:
                rounded[c] = sb(f"g_bf16_{c}{z}", [P, TILE * PACK], BF16)
                if scalar_helps and c % 2 == 1:
                    nc.scalar.copy(out=by_word(rounded[c][:]), in_=by_row(g_raw[z][c]))
                else:
                    nc.vector.tensor_copy(out=by_word(rounded[c][:]), in_=by_row(g_raw[z][c]))
            for c in tiles:
                g_codes[c, z] = sb(f"g_codes_{c}{z}", [P, TILE], U32)
                g_scale[c, z] = sb(f"g_scale_{c}{z}", [P, TILE], U8)
                nc.vector.quantize_mx(out=g_codes[c, z][:].bitcast(E5M2), scales=g_scale[c, z][:], in_=rounded[c][:])

        def first_product(c, z):
            if z == 0:
                dt_psum[c] = bank(f"dt_{c}", c)
            nc.tensor.matmul_mx(
                out=dt_psum[c][:],
                lhsT=g_codes[c, z][:].bitcast(E5M2),
                lhsT_scale=g_scale[c, z][:],
                rhs=wd[:, cols(z, R * FP4_BYTES)].bitcast(E2M1),
                rhs_scale=wd_scale[:, cols(z, R)],
                start=(z == 0),
                stop=(z == PASSES - 1),
            )

        def copy_out_dt(c):
            dt_sbuf[c] = sb(f"dt_sbuf_{c}", [P, PACK, P], F32)
            nc.scalar.copy(out=dt_sbuf[c][:], in_=dt_psum[c][:].rearrange("t (m j) -> t j m", j=PACK))

        def transpose_dt(c):
            d_psum[c] = bank(f"d_{c}", TILES + c)
            for j in range(PACK):
                nc.tensor.transpose(d_psum[c][:, cols(j, TILE)], dt_sbuf[c][:, j, :], identity[:])

        quantise_g(range(TILES), 0, scalar_helps=True)
        for c in range(TILES - 1):
            first_product(c, 0)
        quantise_g((0, 1), 1, scalar_helps=True)
        first_product(0, 1)
        first_product(1, 1)
        first_product(TILES - 1, 0)
        copy_out_dt(0)
        copy_out_dt(1)
        quantise_g((2, 3), 1, scalar_helps=False)
        transpose_dt(0)
        transpose_dt(1)
        first_product(2, 1)
        first_product(3, 1)
        copy_out_dt(2)
        copy_out_dt(3)

        da_bf16 = sb("da_bf16", [P, T * PACK], BF16)
        db_bf16 = sb("db_bf16", [P, T * PACK], BF16)

        def multiply(product, factor, c):
            nc.vector.tensor_tensor(
                out=by_word(product[:, cols(c, TILE * PACK)]),
                in0=by_row(d_psum[c][:].rearrange("p (j t) -> p j t", j=PACK)),
                in1=by_row(factor[c]),
                op=mybir.AluOpType.mult,
            )

        def quantise_da(first_token, tokens):
            first = first_token + (first_token // HALF + 1) * HALF
            nc.vector.quantize_mx(
                out=da_codes[:, first : first + tokens].bitcast(E5M2),
                scales=da_scale[:, first : first + tokens],
                in_=da_bf16[:, first_token * PACK : (first_token + tokens) * PACK],
            )

        def quantise_db(first_token, tokens):
            nc.vector.quantize_mx(
                out=db_codes[:, first_token : first_token + tokens].bitcast(E4M3),
                scales=db_scale[:, first_token : first_token + tokens],
                in_=db_bf16[:, first_token * PACK : (first_token + tokens) * PACK],
            )

        def product_a(acc, side, half, kt, start):
            first = (2 * half + 1 - side) * HALF
            window = slice(first, first + BANK)
            nc.tensor.matmul_mx(
                out=acc[:],
                lhsT=wa[:, cols(kt, P)].bitcast(E4M3),
                lhsT_scale=wa_scale[:, cols(kt, P)],
                rhs=da_codes[:, window].bitcast(E5M2),
                rhs_scale=da_scale[:, window],
                start=start,
                stop=False,
            )

        def product_b(acc, side, c, kt, stop):
            first = side * HALF + (c % 2) * TILE
            nc.tensor.matmul_mx(
                out=acc[:, first : first + TILE],
                lhsT=wb[:, cols(kt, P * FP4_BYTES)].bitcast(E2M1),
                lhsT_scale=wb_scale[:, cols(kt, P)],
                rhs=db_codes[:, cols(c, TILE)].bitcast(E4M3),
                rhs_scale=db_scale[:, cols(c, TILE)],
                start=False,
                stop=stop,
            )

        out_rows = out.rearrange("(kt p) t -> p kt t", p=P)

        multiply(da_bf16, gs_raw, 0)
        multiply(da_bf16, gs_raw, 1)
        transpose_dt(2)
        transpose_dt(3)
        multiply(db_bf16, zs_raw, 0)
        multiply(db_bf16, zs_raw, 1)
        quantise_da(0, HALF)
        quantise_db(0, HALF)

        first_sums = [bank(f"first_sum_{b}", b) for b in range(2)]
        for b in range(2):
            for side in range(2):
                product_a(first_sums[b], side, 0, 2 * b + side, start=(side == 0))
        for b in range(2):
            for c in (0, 1):
                for side in range(2):
                    product_b(first_sums[b], side, c, 2 * b + side, stop=(c == 1 and side == 1))
        for b in range(2):
            result = sb(f"first_result_{b}", [P, BANK], F32)
            nc.scalar.copy(out=result[:], in_=first_sums[b][:])
            nc.sync.dma_start(
                out=out_rows[:, cols(b, 2), cols(0, HALF)], in_=result[:].rearrange("p (kt t) -> p kt t", kt=2)
            )

        multiply(da_bf16, gs_raw, 2)
        multiply(da_bf16, gs_raw, 3)
        quantise_da(2 * TILE, TILE)
        quantise_da(3 * TILE, TILE)
        multiply(db_bf16, zs_raw, 2)

        second_sums = [bank(f"second_sum_{kt}", 2 + kt) for kt in range(K // P)]
        for kt, acc in enumerate(second_sums):
            product_a(acc, 1, 1, kt, start=True)
        multiply(db_bf16, zs_raw, 3)
        quantise_db(2 * TILE, TILE)
        quantise_db(3 * TILE, TILE)
        for kt, acc in enumerate(second_sums):
            product_b(acc, 1, 2, kt, stop=False)
            product_b(acc, 1, 3, kt, stop=True)
        for kt, acc in enumerate(second_sums):
            result = sb(f"second_result_{kt}", [P, HALF], F32)
            if kt % 2 == 0:
                nc.scalar.copy(out=result[:], in_=acc[:, cols(1, HALF)])
            else:
                nc.vector.tensor_copy(out=result[:], in_=acc[:, cols(1, HALF)])
            nc.sync.dma_start(out=out_rows[:, kt, cols(1, HALF)], in_=result[:])
